import numpy as np
import ml_dtypes

BF16 = ml_dtypes.bfloat16


def bf(x):
    return np.asarray(x, np.float32).astype(BF16)


def f32(x):
    return np.asarray(x, np.float32)


def f64(x):
    return np.asarray(x).astype(np.float64)


def striped(idx):
    return np.tile(idx.reshape(-1, 16).T, (8, 1))


def rows(idx, k):
    return np.tile(idx, (k, 1))


def look(tab, idx):
    return np.take_along_axis(f64(tab), rows(idx, len(tab)), axis=1)


K, S, D, V, N = 256, 256, 1, 256, 256


def setup_inputs():
    return {"tab": bf(0.7 * np.random.standard_normal((D, K, S))), "base": bf(np.random.standard_normal((K, V))), "offs": striped(np.random.randint(0, S, N))}


def reference(tab, base, offs):
    idx = offs[:16].T.reshape(-1)
    x = f64(base) + sum(look(tab[d], idx[d * V:(d + 1) * V]) for d in range(D))
    return x

@@ -1,0 +1,38 @@
+import concourse.mybir as mybir
+
+BF16, F32, U16 = mybir.dt.bfloat16, mybir.dt.float32, mybir.dt.uint16
+ADD = mybir.AluOpType.add
+
+P = 128
+SLOTS = 2
+S = 256
+V = 256
+
+
+def tile_lookup_res_add_out_kernel(tc, tab, base, offs, out):
+    nc = tc.nc
+    tab_rows = tab[0].rearrange("(p b) s -> p (b s)", b=SLOTS)
+    base_rows = base.rearrange("(p b) v -> p (b v)", b=SLOTS)
+    out_rows = out.rearrange("(p b) v -> p b v", b=SLOTS)
+
+    with tc.tile_pool(name="held", bufs=1) as held:
+        offsets = held.tile([P, V // 16], U16, name="offsets")
+        tab_bf16 = held.tile([P, SLOTS * S], BF16, name="tab_bf16")
+        base_bf16 = held.tile([P, SLOTS * V], BF16, name="base_bf16")
+        nc.sync.dma_start(tab_bf16[:], tab_rows)
+        nc.scalar.dma_start(base_bf16[:], base_rows)
+        nc.sync.dma_start(offsets[:], offs)
+
+        windows, bases = [], []
+        for b in range(SLOTS):
+            window = held.tile([P, S], F32, name=f"window{b}")
+            nc.vector.tensor_copy(window[:], tab_bf16[:, b * S : (b + 1) * S])
+            windows.append(window)
+            base_f32 = held.tile([P, V], F32, name=f"base_f32_{b}")
+            nc.scalar.copy(base_f32[:], base_bf16[:, b * V : (b + 1) * V])
+            bases.append(base_f32)
+
+        for b in range(SLOTS):
+            x = held.tile([P, V], F32, name=f"x{b}")
+            nc.vector.tensor_tensor(x[:], windows[b][:].indirect(offsets[:]), bases[b][:], ADD)
+            nc.sync.dma_start(out_rows[:, b, :], x[:])

@@ -23,14 +23,12 @@ def tile_lookup_res_add_out_kernel(tc, tab, base, offs, out):
         nc.scalar.dma_start(base_bf16[:], base_rows)
         nc.sync.dma_start(offsets[:], offs)
 
-        windows, bases = [], []
-        for b in range(SLOTS):
-            window = held.tile([P, S], F32, name=f"window{b}")
-            nc.vector.tensor_copy(window[:], tab_bf16[:, b * S : (b + 1) * S])
-            windows.append(window)
-            base_f32 = held.tile([P, V], F32, name=f"base_f32_{b}")
-            nc.scalar.copy(base_f32[:], base_bf16[:, b * V : (b + 1) * V])
-            bases.append(base_f32)
+        windows = [held.tile([P, S], F32, name=f"window{b}") for b in range(SLOTS)]
+        bases = [held.tile([P, V], F32, name=f"base_f32_{b}") for b in range(SLOTS)]
+        nc.vector.tensor_copy(windows[0][:], tab_bf16[:, 0:S])
+        nc.vector.tensor_copy(bases[0][:], base_bf16[:, 0:V])
+        nc.scalar.copy(windows[1][:], tab_bf16[:, S : 2 * S])
+        nc.scalar.copy(bases[1][:], base_bf16[:, V : 2 * V])
 
         for b in range(SLOTS):
             x = held.tile([P, V], F32, name=f"x{b}")

@@ -4,33 +4,35 @@ BF16, F32, U16 = mybir.dt.bfloat16, mybir.dt.float32, mybir.dt.uint16
 ADD = mybir.AluOpType.add
 
 P = 128
-SLOTS = 2
+BLOCKS = 2
 S = 256
 V = 256
 
 
 def tile_lookup_res_add_out_kernel(tc, tab, base, offs, out):
     nc = tc.nc
-    tab_rows = tab[0].rearrange("(p b) s -> p (b s)", b=SLOTS)
-    base_rows = base.rearrange("(p b) v -> p (b v)", b=SLOTS)
-    out_rows = out.rearrange("(p b) v -> p b v", b=SLOTS)
+    tab_blocks = tab[0].rearrange("(b p) s -> b p s", p=P)
+    base_blocks = base.rearrange("(b p) v -> b p v", p=P)
+    out_blocks = out.rearrange("(b p) v -> b p v", p=P)
 
     with tc.tile_pool(name="held", bufs=1) as held:
         offsets = held.tile([P, V // 16], U16, name="offsets")
-        tab_bf16 = held.tile([P, SLOTS * S], BF16, name="tab_bf16")
-        base_bf16 = held.tile([P, SLOTS * V], BF16, name="base_bf16")
-        nc.sync.dma_start(tab_bf16[:], tab_rows)
-        nc.scalar.dma_start(base_bf16[:], base_rows)
+        tabs_bf16 = [held.tile([P, S], BF16, name=f"tab_bf16_{b}") for b in range(BLOCKS)]
+        bases_bf16 = [held.tile([P, V], BF16, name=f"base_bf16_{b}") for b in range(BLOCKS)]
+        nc.sync.dma_start(tabs_bf16[0][:], tab_blocks[0])
+        nc.scalar.dma_start(bases_bf16[0][:], base_blocks[0])
         nc.sync.dma_start(offsets[:], offs)
+        nc.scalar.dma_start(tabs_bf16[1][:], tab_blocks[1])
+        nc.sync.dma_start(bases_bf16[1][:], base_blocks[1])
 
-        windows = [held.tile([P, S], F32, name=f"window{b}") for b in range(SLOTS)]
-        bases = [held.tile([P, V], F32, name=f"base_f32_{b}") for b in range(SLOTS)]
-        nc.vector.tensor_copy(windows[0][:], tab_bf16[:, 0:S])
-        nc.vector.tensor_copy(bases[0][:], base_bf16[:, 0:V])
-        nc.scalar.copy(windows[1][:], tab_bf16[:, S : 2 * S])
-        nc.scalar.copy(bases[1][:], base_bf16[:, V : 2 * V])
+        windows = [held.tile([P, S], F32, name=f"window{b}") for b in range(BLOCKS)]
+        bases = [held.tile([P, V], F32, name=f"base_f32_{b}") for b in range(BLOCKS)]
+        nc.vector.tensor_copy(windows[0][:], tabs_bf16[0][:])
+        nc.vector.tensor_copy(bases[0][:], bases_bf16[0][:])
+        nc.scalar.copy(windows[1][:], tabs_bf16[1][:])
+        nc.scalar.copy(bases[1][:], bases_bf16[1][:])
 
-        for b in range(SLOTS):
+        for b in range(BLOCKS):
             x = held.tile([P, V], F32, name=f"x{b}")
             nc.vector.tensor_tensor(x[:], windows[b][:].indirect(offsets[:]), bases[b][:], ADD)
-            nc.sync.dma_start(out_rows[:, b, :], x[:])
+            nc.sync.dma_start(out_blocks[b], x[:])

import concourse.mybir as mybir

BF16, F32, U16 = mybir.dt.bfloat16, mybir.dt.float32, mybir.dt.uint16
ADD = mybir.AluOpType.add

P = 128
BLOCKS = 2
S = 256
V = 256


def tile_lookup_res_add_out_kernel(tc, tab, base, offs, out):
    nc = tc.nc
    tab_blocks = tab[0].rearrange("(b p) s -> b p s", p=P)
    base_blocks = base.rearrange("(b p) v -> b p v", p=P)
    out_blocks = out.rearrange("(b p) v -> b p v", p=P)

    with tc.tile_pool(name="held", bufs=1) as held:
        offsets = held.tile([P, V // 16], U16, name="offsets")
        tabs_bf16 = [held.tile([P, S], BF16, name=f"tab_bf16_{b}") for b in range(BLOCKS)]
        bases_bf16 = [held.tile([P, V], BF16, name=f"base_bf16_{b}") for b in range(BLOCKS)]
        nc.sync.dma_start(tabs_bf16[0][:], tab_blocks[0])
        nc.scalar.dma_start(bases_bf16[0][:], base_blocks[0])
        nc.sync.dma_start(offsets[:], offs)
        nc.scalar.dma_start(tabs_bf16[1][:], tab_blocks[1])
        nc.sync.dma_start(bases_bf16[1][:], base_blocks[1])

        windows = [held.tile([P, S], F32, name=f"window{b}") for b in range(BLOCKS)]
        bases = [held.tile([P, V], F32, name=f"base_f32_{b}") for b in range(BLOCKS)]
        nc.vector.tensor_copy(windows[0][:], tabs_bf16[0][:])
        nc.vector.tensor_copy(bases[0][:], bases_bf16[0][:])
        nc.scalar.copy(windows[1][:], tabs_bf16[1][:])
        nc.scalar.copy(bases[1][:], bases_bf16[1][:])

        for b in range(BLOCKS):
            x = held.tile([P, V], F32, name=f"x{b}")
            nc.vector.tensor_tensor(x[:], windows[b][:].indirect(offsets[:]), bases[b][:], ADD)
            nc.sync.dma_start(out_blocks[b], x[:])
